import numpy as np
import ml_dtypes


def mxq(x, axis, fmt="e4m3"):
    dtype, down = {"e4m3": (ml_dtypes.float8_e4m3fn, 7), "e5m2": (ml_dtypes.float8_e5m2, 14)}[fmt]
    v = np.moveaxis(np.asarray(x, np.float32).astype(ml_dtypes.bfloat16).astype(np.float64), axis, -1)
    blocks = v.reshape(v.shape[:-1] + (-1, 32))
    amax = np.abs(blocks).max(-1, keepdims=True)
    byte = np.maximum(np.where(amax > 0, np.frexp(amax)[1] - 1 + 127, 0) - down, 1)
    scale = np.exp2(byte - 127.0)
    codes = (blocks / scale).astype(np.float32).astype(dtype).astype(np.float64)
    return np.moveaxis((codes * scale).reshape(v.shape), -1, axis)


WIDE = False


def mx_kscale(k):
    if not WIDE:
        return np.ones(k)
    levels = np.array([24, -24, 12, -12, 0])
    if k % 512:
        return np.exp2(np.random.permutation(np.resize(levels, k // 32))).repeat(32)
    a = np.empty((k // 512, 16))
    for p in range(k // 512):
        a[p, :8] = np.random.permutation(np.resize(levels, 8))
        for g in range(8):
            far = levels[np.abs(levels - a[p, g]) >= 10]
            a[p, g + 8] = far[np.random.randint(len(far))]
    return np.exp2(a.ravel()).repeat(32)


def f64(x):
    return np.asarray(x).astype(np.float64)


def striped8(idx):
    return np.concatenate([v.reshape(-1, 16).T for v in idx]).astype(np.uint16)


def unstriped8(offs):
    return np.stack([offs[16 * g:16 * g + 16].T.reshape(-1) for g in range(8)]).astype(np.int64)


E2M1 = np.array([0.0, 0.5, 1.0, 1.5, 2.0, 3.0, 4.0, 6.0, -0.0, -0.5, -1.0, -1.5, -2.0, -3.0, -4.0, -6.0])


def pack_weight(w, fmt):
    k, n = w.shape
    w = f64(np.asarray(w, np.float32).astype(ml_dtypes.bfloat16)).reshape(k // 32, 32, n)
    amax = np.abs(w).max(1)
    if fmt == "e4m3":
        byte = np.frexp(amax)[1] - 1 + 127 - 7
    else:
        mant, ex = np.frexp(amax / 6.0)
        byte = np.where(mant > 0.5, ex, ex - 1) + 127
    byte = np.clip(np.where(amax > 0, byte, 1), 1, 254)
    scaled = (w * np.exp2(127.0 - byte)[:, None, :]).reshape(k, n).astype(np.float32)
    by_word = np.ascontiguousarray(scaled.reshape(k // 512, 128, 4, n).transpose(0, 1, 3, 2))
    if fmt == "e4m3":
        words = by_word.astype(ml_dtypes.float8_e4m3fn).view(np.uint8)
    else:
        c = by_word.astype(ml_dtypes.float4_e2m1fn).view(np.uint8) & 0xF
        words = (c[..., 0::2] | (c[..., 1::2] << 4)).reshape(k // 512, 128, 2 * n)
    return np.ascontiguousarray(words), np.ascontiguousarray(byte.astype(np.uint8).reshape(k // 512, 16, n))


def unpack_weight(words, scales, fmt):
    g, _, n = scales.shape
    words = np.ascontiguousarray(words).reshape(g, 128, n, -1)
    if fmt == "e4m3":
        vals = words.view(ml_dtypes.float8_e4m3fn).astype(np.float64)
    else:
        nib = np.empty((g, 128, n, 4), np.uint8)
        nib[..., 0::2] = words & 0xF
        nib[..., 1::2] = words >> 4
        vals = E2M1[nib]
    vals = vals * np.repeat(np.exp2(scales.astype(np.float64) - 127.0), 8, axis=1)[..., None]
    return vals.transpose(0, 1, 3, 2).reshape(g * 512, n)


def planes(y):
    n, m = y.shape
    v = y.astype(np.float32).astype(ml_dtypes.bfloat16).astype(np.float64).reshape(n // 32, 32, m)
    top = np.abs(v).max(1)
    byte = np.clip(np.where(top > 0, np.frexp(top)[1] - 1 + 127 - 7, 1), 1, 254)
    codes = (v * np.exp2(127.0 - byte)[:, None, :]).reshape(n, m).astype(np.float32).astype(ml_dtypes.float8_e4m3fn).view(np.uint8)
    words = codes.reshape(n // 512, 128, 4, m).transpose(0, 1, 3, 2)
    return np.ascontiguousarray(words), np.ascontiguousarray(byte.astype(np.uint8).reshape(n // 512, 16, m))


K, L, N, T, J = 512, 512, 512, 2048, 1024


def setup_inputs():
    n = np.random.standard_normal
    s = mx_kscale(K)[:, None]
    s2 = mx_kscale(L)[:, None]
    p_wb = pack_weight(n((L, N)) / np.sqrt(L) / s2, "e4m3")
    return {
        "xT": (n((K, T)) * s).astype(np.float32),
        "wgt": np.repeat(np.random.uniform(0.5, 2.0, (8, J)), 16, axis=0).astype(np.float32),
        "zT": (n((L, T)) * s2).astype(np.float32),
        "wgt2": np.repeat(np.random.uniform(0.5, 2.0, (8, J)), 16, axis=0).astype(np.float32),
        "wa": (n((K, N)) / np.sqrt(K) / s).astype(np.float32),
        "wb_words": p_wb[0],
        "wb_scales": p_wb[1],
        "b": (0.3 * n(N)).astype(np.float32),
        "offs": striped8(np.stack([np.random.permutation(T)[:J] for _ in range(8)])),
        "offs2": striped8(np.stack([np.random.permutation(T)[:J] for _ in range(8)])),
    }


def reference(xT, wgt, zT, wgt2, wa, wb_words, wb_scales, b, offs, offs2):
    idx = unstriped8(offs)
    idx2 = unstriped8(offs2)
    rows = np.arange(K)
    xg = f64(wgt)[rows // 4 % 128] * f64(xT)[rows[:, None], idx[rows % 512 // 64]]
    xT_ = mxq(xg, 0, "e4m3")
    rows = np.arange(L)
    xg = f64(wgt2)[rows // 4 % 128] * f64(zT)[rows[:, None], idx2[rows % 512 // 64]]
    zT_ = mxq(xg, 0, "e4m3")
    wa_ = mxq(f64(wa), 0, "e4m3")
    wb_ = unpack_weight(wb_words, wb_scales, "e4m3")
    ya = wa_.T @ xT_
    yb = wb_.T @ zT_
    out_0 = np.maximum(ya, yb) + f64(b)[:, None]
    return (out_0,) + planes(out_0)

@@ -1,0 +1,220 @@
+from contextlib import ExitStack
+
+import concourse.mybir as mybir
+
+K, N, T, J = 512, 512, 2048, 1024
+FLOPS = 2 * 2 * K * N * J
+
+F32 = mybir.dt.float32
+BF16 = mybir.dt.bfloat16
+I32 = mybir.dt.int32
+U32 = mybir.dt.uint32
+U16 = mybir.dt.uint16
+U8 = mybir.dt.uint8
+FP8X4 = mybir.dt.float8_e4m3fn_x4
+ALU = mybir.AluOpType
+ACT = mybir.ActivationFunctionType
+
+P = 128
+PACK = 4
+BANK = 512
+Z_CHUNKS = [(0, 512), (512, 512)]
+HEAD_CHUNKS = [(0, 256), (256, 768)]
+X_CHUNKS = [(0, 256), (256, 256), (512, 256), (768, 128), (896, 128)]
+
+
+def tile_list_max_biasP_kernel(
+    tc, xT, wgt, zT, wgt2, wa, wb_words, wb_scales, b, offs, offs2, out_0, out_1, out_2
+):
+    nc = tc.nc
+    with ExitStack() as ctx:
+        keep = ctx.enter_context(tc.tile_pool(name="keep", bufs=1))
+        psum = ctx.enter_context(tc.psum_pool(name="psum", bufs=8))
+
+        def sb(name, shape, dtype, tag=None):
+            return keep.tile(shape, dtype, name=name, tag=tag or name, align_bytes=64)
+
+        z_list = keep.tile([P, J // 16], U16, name="z_list")
+        x_list = keep.tile([P, J // 16], U16, name="x_list")
+        z_planes = [sb("z_plane%d" % i, [P, T], F32) for i in range(PACK)]
+        x_planes = [sb("x_plane%d" % i, [P, T], F32) for i in range(PACK)]
+        z_wgt = sb("z_wgt", [P, J], F32)
+        x_wgt = sb("x_wgt", [P, J], F32)
+        wa_raw = [sb("wa_raw%d" % h, [P, PACK, N // 2], F32) for h in range(2)]
+        wb_raw = sb("wb_raw", [P, N], I32)
+        wb_raw_scales = sb("wb_raw_scales", [P, N], U8)
+        bias = sb("bias", [P, PACK], F32)
+        z_rows = zT.rearrange("(p i) t -> p i t", i=PACK)
+        x_rows = xT.rearrange("(p i) t -> p i t", i=PACK)
+        wa_rows = wa.rearrange("(p i) n -> p i n", i=PACK)
+
+        nc.gpsimd.memset(wb_raw_scales[:].bitcast(I32), 0)
+        nc.sync.dma_start(z_list[:], offs2)
+        nc.sync.dma_start(z_planes[0][:], z_rows[:, 0, :])
+        for q in range(4):
+            nc.gpsimd.dma_start(
+                wb_raw_scales[32 * q : 32 * q + 4, :].bitcast(I32),
+                wb_scales[0, 4 * q : 4 * q + 4, :].bitcast(I32),
+            )
+        for j0, n in HEAD_CHUNKS:
+            nc.sync.dma_start(z_wgt[:, j0 : j0 + n], wgt2[:, j0 : j0 + n])
+        for i in range(1, PACK):
+            nc.sync.dma_start(z_planes[i][:], z_rows[:, i, :])
+        nc.sync.dma_start(wb_raw[:], wb_words[0].rearrange("p n i -> p (n i)").bitcast(I32))
+        nc.sync.dma_start(x_list[:], offs)
+        nc.sync.dma_start(bias[:], b.rearrange("(p t) -> p t", t=PACK))
+        nc.sync.dma_start(x_wgt[:], wgt)
+        nc.sync.dma_start(x_planes[0][:], x_rows[:, 0, :])
+        nc.sync.dma_start(x_planes[1][:], x_rows[:, 1, :])
+        nc.sync.dma_start(wa_raw[0][:], wa_rows[:, :, : N // 2])
+        nc.sync.dma_start(x_planes[2][:], x_rows[:, 2, :])
+        nc.sync.dma_start(wa_raw[1][:], wa_rows[:, :, N // 2 :])
+        nc.sync.dma_start(x_planes[3][:], x_rows[:, 3, :])
+
+        wb_codes = sb("wb_codes", [P, N], I32)
+        wb_sc = sb("wb_sc", [P, N], U8)
+        nc.vector.tensor_copy(
+            wb_codes[:].rearrange("p (t m) -> p m t", t=PACK), wb_raw[:].rearrange("p (m t) -> p m t", t=PACK)
+        )
+        nc.vector.tensor_copy(
+            wb_sc[:].rearrange("p (t m) -> p m t", t=PACK), wb_raw_scales[:].rearrange("p (m t) -> p m t", t=PACK)
+        )
+
+        def gather(dst, plane, offsets, weights, j0, n):
+            nc.vector.tensor_tensor(
+                dst, plane[:].indirect(offsets[:, j0 // 16 : (j0 + n) // 16]), weights, ALU.mult
+            )
+
+        def weave(dst, src):
+            nc.scalar.activation(
+                dst[:].rearrange("p (c i) t -> p c t i", i=4),
+                src.rearrange("p t (c i) -> p c t i", i=4),
+                ACT.Copy,
+            )
+
+        def quantize(codes, scales, src):
+            nc.vector.quantize_mx(codes.bitcast(FP8X4), scales, src[:].rearrange("p j t -> p (j t)"))
+
+        z_picked = sb("z_picked", [P, PACK, J], F32)
+        for i, pieces in enumerate([HEAD_CHUNKS, [(0, J)], [(0, J)], Z_CHUNKS]):
+            for j0, n in pieces:
+                gather(z_picked[:, i, j0 : j0 + n], z_planes[i], z_list, z_wgt[:, j0 : j0 + n], j0, n)
+        z_ops = []
+        for c, (j0, n) in enumerate(Z_CHUNKS):
+            woven = sb("z_woven%d" % c, [P, n, PACK], BF16)
+            codes = sb("z_codes%d" % c, [P, n], U32)
+            scales = sb("z_scales%d" % c, [P, n], U8)
+            weave(woven, z_picked[:, :, j0 : j0 + n])
+            quantize(codes[:], scales[:], woven)
+            z_ops.append((codes, scales))
+        wa_woven = sb("wa_woven", [P, N, PACK], BF16)
+        wa_codes = sb("wa_codes", [P, N], U32)
+        wa_sc = sb("wa_sc", [P, N], U8)
+        for h in range(2):
+            nc.scalar.activation(
+                wa_woven[:].rearrange("p (t m) i -> p m i t", t=PACK)[:, 64 * h : 64 * (h + 1)],
+                wa_raw[h][:].rearrange("p i (m t) -> p m i t", t=PACK),
+                ACT.Copy,
+            )
+        quantize(wa_codes[:], wa_sc[:], wa_woven)
+        yb = {}
+        for c, (j0, n) in enumerate(Z_CHUNKS):
+            for t0 in (0, 2):
+                late = c == 1 and t0 == 2
+                pair = sb("yb%d_%d" % (c, t0), [P, 2, n], F32, tag="wa_raw1" if late else None)
+                yb[c, t0], yb[c, t0 + 1] = pair[:, 0, :], pair[:, 1, :]
+
+        def yb_pieces(t, j0, n):
+            return [
+                (max(j0, z0), min(j0 + n, z0 + zn), yb[c, t][:, max(j0, z0) - z0 : min(j0 + n, z0 + zn) - z0])
+                for c, (z0, zn) in enumerate(Z_CHUNKS)
+                if max(j0, z0) < min(j0 + n, z0 + zn)
+            ]
+
+        for c, (j0, n) in enumerate(Z_CHUNKS):
+            codes, scales = z_ops[c]
+            for t in range(PACK):
+                acc = psum.tile([P, BANK], F32, name="acc")
+                nc.tensor.matmul_mx(
+                    acc[:, :n],
+                    lhsT=wb_codes[:, P * t : P * (t + 1)].bitcast(FP8X4),
+                    lhsT_scale=wb_sc[:, P * t : P * (t + 1)],
+                    rhs=codes[:].bitcast(FP8X4),
+                    rhs_scale=scales[:],
+                    start=True,
+                    stop=True,
+                )
+                nc.scalar.activation(yb[c, t], acc[:, :n], ACT.Identity, bias=bias[:, t : t + 1])
+
+        x_picked = sb("x_picked", [P, PACK, J], F32)
+        for i in range(PACK - 1):
+            gather(x_picked[:, i, :], x_planes[i], x_list, x_wgt[:], 0, J)
+        for j0, n in X_CHUNKS:
+            gather(x_picked[:, PACK - 1, j0 : j0 + n], x_planes[PACK - 1], x_list, x_wgt[:, j0 : j0 + n], j0, n)
+
+        out_rows = out_0.rearrange("(p t) j -> p t j", t=PACK)
+        out_words = out_1[0].rearrange("p j i -> p (j i)").bitcast(I32)
+        y_scales = sb("y_scales", [P, J], U8)
+        x_ops = {}
+        y_tiles = {}
+
+        def x_quantize(c):
+            j0, n = X_CHUNKS[c]
+            woven = sb("x_woven%d" % c, [P, n, PACK], BF16)
+            codes = sb("x_codes%d" % c, [P, n], U32)
+            scales = sb("x_scales%d" % c, [P, n], U8)
+            weave(woven, x_picked[:, :, j0 : j0 + n])
+            quantize(codes[:], scales[:], woven)
+            x_ops[c] = (codes, scales)
+
+        def combine(c):
+            j0, n = X_CHUNKS[c]
+            codes, scales = x_ops[c]
+            y = sb("y%d" % c, [P, PACK, n], F32)
+            per_bank = min(PACK, BANK // n)
+            for t0 in range(0, PACK, per_bank):
+                acc = psum.tile([P, BANK], F32, name="acc")
+                for t in range(t0, t0 + per_bank):
+                    nc.tensor.matmul_mx(
+                        acc[:, (t - t0) * n : (t - t0 + 1) * n],
+                        lhsT=wa_codes[:, P * t : P * (t + 1)].bitcast(FP8X4),
+                        lhsT_scale=wa_sc[:, P * t : P * (t + 1)],
+                        rhs=codes[:].bitcast(FP8X4),
+                        rhs_scale=scales[:],
+                        start=True,
+                        stop=True,
+                    )
+                for t in range(t0, t0 + per_bank):
+                    for lo, hi, other in yb_pieces(t, j0, n):
+                        nc.vector.scalar_tensor_tensor(
+                            y[:, t, lo - j0 : hi - j0],
+                            acc[:, (t - t0) * n + lo - j0 : (t - t0) * n + hi - j0],
+                            bias[:, t : t + 1],
+                            other,
+                            ALU.add,
+                            ALU.max,
+                        )
+            nc.sync.dma_start(out_rows[:, :, j0 : j0 + n], y[:])
+            y_tiles[c] = y
+
+        def y_quantize(c):
+            j0, n = X_CHUNKS[c]
+            woven = sb("y_woven%d" % c, [P, n, PACK], BF16)
+            codes = sb("y_codes%d" % c, [P, n], U32)
+            weave(woven, y_tiles[c][:])
+            quantize(codes[:], y_scales[:, j0 : j0 + n], woven)
+            nc.sync.dma_start(out_words[:, j0 : j0 + n], codes[:].bitcast(I32))
+
+        chunks = len(X_CHUNKS)
+        for step in range(chunks + 2):
+            if step < chunks:
+                x_quantize(step)
+            if 0 <= step - 1 < chunks:
+                combine(step - 1)
+            if 0 <= step - 2 < chunks:
+                y_quantize(step - 2)
+        for q in range(4):
+            engine = nc.sync if q % 2 else nc.scalar
+            engine.dma_start(
+                out_2[0, 4 * q : 4 * q + 4, :].bitcast(I32), y_scales[32 * q : 32 * q + 4, :].bitcast(I32)
+            )

@@ -20,6 +20,7 @@ PACK = 4
 BANK = 512
 Z_CHUNKS = [(0, 512), (512, 512)]
 HEAD_CHUNKS = [(0, 256), (256, 768)]
+Z_PIECES = [(0, 256), (256, 256), (512, 512)]
 X_CHUNKS = [(0, 256), (256, 256), (512, 256), (768, 128), (896, 128)]
 
 
@@ -48,11 +49,11 @@ def tile_list_max_biasP_kernel(
         x_rows = xT.rearrange("(p i) t -> p i t", i=PACK)
         wa_rows = wa.rearrange("(p i) n -> p i n", i=PACK)
 
-        nc.gpsimd.memset(wb_raw_scales[:].bitcast(I32), 0)
+        nc.vector.memset(wb_raw_scales[:].bitcast(I32), 0)
         nc.sync.dma_start(z_list[:], offs2)
         nc.sync.dma_start(z_planes[0][:], z_rows[:, 0, :])
         for q in range(4):
-            nc.gpsimd.dma_start(
+            nc.scalar.dma_start(
                 wb_raw_scales[32 * q : 32 * q + 4, :].bitcast(I32),
                 wb_scales[0, 4 * q : 4 * q + 4, :].bitcast(I32),
             )
@@ -71,15 +72,6 @@ def tile_list_max_biasP_kernel(
         nc.sync.dma_start(wa_raw[1][:], wa_rows[:, :, N // 2 :])
         nc.sync.dma_start(x_planes[3][:], x_rows[:, 3, :])
 
-        wb_codes = sb("wb_codes", [P, N], I32)
-        wb_sc = sb("wb_sc", [P, N], U8)
-        nc.vector.tensor_copy(
-            wb_codes[:].rearrange("p (t m) -> p m t", t=PACK), wb_raw[:].rearrange("p (m t) -> p m t", t=PACK)
-        )
-        nc.vector.tensor_copy(
-            wb_sc[:].rearrange("p (t m) -> p m t", t=PACK), wb_raw_scales[:].rearrange("p (m t) -> p m t", t=PACK)
-        )
-
         def gather(dst, plane, offsets, weights, j0, n):
             nc.vector.tensor_tensor(
                 dst, plane[:].indirect(offsets[:, j0 // 16 : (j0 + n) // 16]), weights, ALU.mult
@@ -87,7 +79,7 @@ def tile_list_max_biasP_kernel(
 
         def weave(dst, src):
             nc.scalar.activation(
-                dst[:].rearrange("p (c i) t -> p c t i", i=4),
+                dst.rearrange("p (c i) t -> p c t i", i=4),
                 src.rearrange("p t (c i) -> p c t i", i=4),
                 ACT.Copy,
             )
@@ -96,15 +88,26 @@ def tile_list_max_biasP_kernel(
             nc.vector.quantize_mx(codes.bitcast(FP8X4), scales, src[:].rearrange("p j t -> p (j t)"))
 
         z_picked = sb("z_picked", [P, PACK, J], F32)
-        for i, pieces in enumerate([HEAD_CHUNKS, [(0, J)], [(0, J)], Z_CHUNKS]):
+        for i, pieces in enumerate([HEAD_CHUNKS, [(0, J)], [(0, J)], Z_PIECES]):
             for j0, n in pieces:
                 gather(z_picked[:, i, j0 : j0 + n], z_planes[i], z_list, z_wgt[:, j0 : j0 + n], j0, n)
+        wb_codes = sb("wb_codes", [P, N], I32)
+        wb_sc = sb("wb_sc", [P, N], U8, tag="z_plane3")
+        nc.vector.tensor_copy(
+            wb_codes[:].rearrange("p (t m) -> p m t", t=PACK), wb_raw[:].rearrange("p (m t) -> p m t", t=PACK)
+        )
+        nc.vector.tensor_copy(
+            wb_sc[:].rearrange("p (t m) -> p m t", t=PACK), wb_raw_scales[:].rearrange("p (m t) -> p m t", t=PACK)
+        )
+
         z_ops = []
         for c, (j0, n) in enumerate(Z_CHUNKS):
             woven = sb("z_woven%d" % c, [P, n, PACK], BF16)
             codes = sb("z_codes%d" % c, [P, n], U32)
             scales = sb("z_scales%d" % c, [P, n], U8)
-            weave(woven, z_picked[:, :, j0 : j0 + n])
+            for p0, pn in Z_PIECES:
+                if j0 <= p0 < j0 + n:
+                    weave(woven[:, p0 - j0 : p0 - j0 + pn, :], z_picked[:, :, p0 : p0 + pn])
             quantize(codes[:], scales[:], woven)
             z_ops.append((codes, scales))
         wa_woven = sb("wa_woven", [P, N, PACK], BF16)
@@ -163,7 +166,7 @@ def tile_list_max_biasP_kernel(
             woven = sb("x_woven%d" % c, [P, n, PACK], BF16)
             codes = sb("x_codes%d" % c, [P, n], U32)
             scales = sb("x_scales%d" % c, [P, n], U8)
-            weave(woven, x_picked[:, :, j0 : j0 + n])
+            weave(woven[:], x_picked[:, :, j0 : j0 + n])
             quantize(codes[:], scales[:], woven)
             x_ops[c] = (codes, scales)
 
@@ -201,7 +204,7 @@ def tile_list_max_biasP_kernel(
             j0, n = X_CHUNKS[c]
             woven = sb("y_woven%d" % c, [P, n, PACK], BF16)
             codes = sb("y_codes%d" % c, [P, n], U32)
-            weave(woven, y_tiles[c][:])
+            weave(woven[:], y_tiles[c][:])
             quantize(codes[:], y_scales[:, j0 : j0 + n], woven)
             nc.sync.dma_start(out_words[:, j0 : j0 + n], codes[:].bitcast(I32))
 

from contextlib import ExitStack

import concourse.mybir as mybir

K, N, T, J = 512, 512, 2048, 1024
FLOPS = 2 * 2 * K * N * J

F32 = mybir.dt.float32
BF16 = mybir.dt.bfloat16
I32 = mybir.dt.int32
U32 = mybir.dt.uint32
U16 = mybir.dt.uint16
U8 = mybir.dt.uint8
FP8X4 = mybir.dt.float8_e4m3fn_x4
ALU = mybir.AluOpType
ACT = mybir.ActivationFunctionType

P = 128
PACK = 4
BANK = 512
Z_CHUNKS = [(0, 512), (512, 512)]
HEAD_CHUNKS = [(0, 256), (256, 768)]
Z_PIECES = [(0, 256), (256, 256), (512, 512)]
X_CHUNKS = [(0, 256), (256, 256), (512, 256), (768, 128), (896, 128)]


def tile_list_max_biasP_kernel(
    tc, xT, wgt, zT, wgt2, wa, wb_words, wb_scales, b, offs, offs2, out_0, out_1, out_2
):
    nc = tc.nc
    with ExitStack() as ctx:
        keep = ctx.enter_context(tc.tile_pool(name="keep", bufs=1))
        psum = ctx.enter_context(tc.psum_pool(name="psum", bufs=8))

        def sb(name, shape, dtype, tag=None):
            return keep.tile(shape, dtype, name=name, tag=tag or name, align_bytes=64)

        z_list = keep.tile([P, J // 16], U16, name="z_list")
        x_list = keep.tile([P, J // 16], U16, name="x_list")
        z_planes = [sb("z_plane%d" % i, [P, T], F32) for i in range(PACK)]
        x_planes = [sb("x_plane%d" % i, [P, T], F32) for i in range(PACK)]
        z_wgt = sb("z_wgt", [P, J], F32)
        x_wgt = sb("x_wgt", [P, J], F32)
        wa_raw = [sb("wa_raw%d" % h, [P, PACK, N // 2], F32) for h in range(2)]
        wb_raw = sb("wb_raw", [P, N], I32)
        wb_raw_scales = sb("wb_raw_scales", [P, N], U8)
        bias = sb("bias", [P, PACK], F32)
        z_rows = zT.rearrange("(p i) t -> p i t", i=PACK)
        x_rows = xT.rearrange("(p i) t -> p i t", i=PACK)
        wa_rows = wa.rearrange("(p i) n -> p i n", i=PACK)

        nc.vector.memset(wb_raw_scales[:].bitcast(I32), 0)
        nc.sync.dma_start(z_list[:], offs2)
        nc.sync.dma_start(z_planes[0][:], z_rows[:, 0, :])
        for q in range(4):
            nc.scalar.dma_start(
                wb_raw_scales[32 * q : 32 * q + 4, :].bitcast(I32),
                wb_scales[0, 4 * q : 4 * q + 4, :].bitcast(I32),
            )
        for j0, n in HEAD_CHUNKS:
            nc.sync.dma_start(z_wgt[:, j0 : j0 + n], wgt2[:, j0 : j0 + n])
        for i in range(1, PACK):
            nc.sync.dma_start(z_planes[i][:], z_rows[:, i, :])
        nc.sync.dma_start(wb_raw[:], wb_words[0].rearrange("p n i -> p (n i)").bitcast(I32))
        nc.sync.dma_start(x_list[:], offs)
        nc.sync.dma_start(bias[:], b.rearrange("(p t) -> p t", t=PACK))
        nc.sync.dma_start(x_wgt[:], wgt)
        nc.sync.dma_start(x_planes[0][:], x_rows[:, 0, :])
        nc.sync.dma_start(x_planes[1][:], x_rows[:, 1, :])
        nc.sync.dma_start(wa_raw[0][:], wa_rows[:, :, : N // 2])
        nc.sync.dma_start(x_planes[2][:], x_rows[:, 2, :])
        nc.sync.dma_start(wa_raw[1][:], wa_rows[:, :, N // 2 :])
        nc.sync.dma_start(x_planes[3][:], x_rows[:, 3, :])

        def gather(dst, plane, offsets, weights, j0, n):
            nc.vector.tensor_tensor(
                dst, plane[:].indirect(offsets[:, j0 // 16 : (j0 + n) // 16]), weights, ALU.mult
            )

        def weave(dst, src):
            nc.scalar.activation(
                dst.rearrange("p (c i) t -> p c t i", i=4),
                src.rearrange("p t (c i) -> p c t i", i=4),
                ACT.Copy,
            )

        def quantize(codes, scales, src):
            nc.vector.quantize_mx(codes.bitcast(FP8X4), scales, src[:].rearrange("p j t -> p (j t)"))

        z_picked = sb("z_picked", [P, PACK, J], F32)
        for i, pieces in enumerate([HEAD_CHUNKS, [(0, J)], [(0, J)], Z_PIECES]):
            for j0, n in pieces:
                gather(z_picked[:, i, j0 : j0 + n], z_planes[i], z_list, z_wgt[:, j0 : j0 + n], j0, n)
        wb_codes = sb("wb_codes", [P, N], I32)
        wb_sc = sb("wb_sc", [P, N], U8, tag="z_plane3")
        nc.vector.tensor_copy(
            wb_codes[:].rearrange("p (t m) -> p m t", t=PACK), wb_raw[:].rearrange("p (m t) -> p m t", t=PACK)
        )
        nc.vector.tensor_copy(
            wb_sc[:].rearrange("p (t m) -> p m t", t=PACK), wb_raw_scales[:].rearrange("p (m t) -> p m t", t=PACK)
        )

        z_ops = []
        for c, (j0, n) in enumerate(Z_CHUNKS):
            woven = sb("z_woven%d" % c, [P, n, PACK], BF16)
            codes = sb("z_codes%d" % c, [P, n], U32)
            scales = sb("z_scales%d" % c, [P, n], U8)
            for p0, pn in Z_PIECES:
                if j0 <= p0 < j0 + n:
                    weave(woven[:, p0 - j0 : p0 - j0 + pn, :], z_picked[:, :, p0 : p0 + pn])
            quantize(codes[:], scales[:], woven)
            z_ops.append((codes, scales))
        wa_woven = sb("wa_woven", [P, N, PACK], BF16)
        wa_codes = sb("wa_codes", [P, N], U32)
        wa_sc = sb("wa_sc", [P, N], U8)
        for h in range(2):
            nc.scalar.activation(
                wa_woven[:].rearrange("p (t m) i -> p m i t", t=PACK)[:, 64 * h : 64 * (h + 1)],
                wa_raw[h][:].rearrange("p i (m t) -> p m i t", t=PACK),
                ACT.Copy,
            )
        quantize(wa_codes[:], wa_sc[:], wa_woven)
        yb = {}
        for c, (j0, n) in enumerate(Z_CHUNKS):
            for t0 in (0, 2):
                late = c == 1 and t0 == 2
                pair = sb("yb%d_%d" % (c, t0), [P, 2, n], F32, tag="wa_raw1" if late else None)
                yb[c, t0], yb[c, t0 + 1] = pair[:, 0, :], pair[:, 1, :]

        def yb_pieces(t, j0, n):
            return [
                (max(j0, z0), min(j0 + n, z0 + zn), yb[c, t][:, max(j0, z0) - z0 : min(j0 + n, z0 + zn) - z0])
                for c, (z0, zn) in enumerate(Z_CHUNKS)
                if max(j0, z0) < min(j0 + n, z0 + zn)
            ]

        for c, (j0, n) in enumerate(Z_CHUNKS):
            codes, scales = z_ops[c]
            for t in range(PACK):
                acc = psum.tile([P, BANK], F32, name="acc")
                nc.tensor.matmul_mx(
                    acc[:, :n],
                    lhsT=wb_codes[:, P * t : P * (t + 1)].bitcast(FP8X4),
                    lhsT_scale=wb_sc[:, P * t : P * (t + 1)],
                    rhs=codes[:].bitcast(FP8X4),
                    rhs_scale=scales[:],
                    start=True,
                    stop=True,
                )
                nc.scalar.activation(yb[c, t], acc[:, :n], ACT.Identity, bias=bias[:, t : t + 1])

        x_picked = sb("x_picked", [P, PACK, J], F32)
        for i in range(PACK - 1):
            gather(x_picked[:, i, :], x_planes[i], x_list, x_wgt[:], 0, J)
        for j0, n in X_CHUNKS:
            gather(x_picked[:, PACK - 1, j0 : j0 + n], x_planes[PACK - 1], x_list, x_wgt[:, j0 : j0 + n], j0, n)

        out_rows = out_0.rearrange("(p t) j -> p t j", t=PACK)
        out_words = out_1[0].rearrange("p j i -> p (j i)").bitcast(I32)
        y_scales = sb("y_scales", [P, J], U8)
        x_ops = {}
        y_tiles = {}

        def x_quantize(c):
            j0, n = X_CHUNKS[c]
            woven = sb("x_woven%d" % c, [P, n, PACK], BF16)
            codes = sb("x_codes%d" % c, [P, n], U32)
            scales = sb("x_scales%d" % c, [P, n], U8)
            weave(woven[:], x_picked[:, :, j0 : j0 + n])
            quantize(codes[:], scales[:], woven)
            x_ops[c] = (codes, scales)

        def combine(c):
            j0, n = X_CHUNKS[c]
            codes, scales = x_ops[c]
            y = sb("y%d" % c, [P, PACK, n], F32)
            per_bank = min(PACK, BANK // n)
            for t0 in range(0, PACK, per_bank):
                acc = psum.tile([P, BANK], F32, name="acc")
                for t in range(t0, t0 + per_bank):
                    nc.tensor.matmul_mx(
                        acc[:, (t - t0) * n : (t - t0 + 1) * n],
                        lhsT=wa_codes[:, P * t : P * (t + 1)].bitcast(FP8X4),
                        lhsT_scale=wa_sc[:, P * t : P * (t + 1)],
                        rhs=codes[:].bitcast(FP8X4),
                        rhs_scale=scales[:],
                        start=True,
                        stop=True,
                    )
                for t in range(t0, t0 + per_bank):
                    for lo, hi, other in yb_pieces(t, j0, n):
                        nc.vector.scalar_tensor_tensor(
                            y[:, t, lo - j0 : hi - j0],
                            acc[:, (t - t0) * n + lo - j0 : (t - t0) * n + hi - j0],
                            bias[:, t : t + 1],
                            other,
                            ALU.add,
                            ALU.max,
                        )
            nc.sync.dma_start(out_rows[:, :, j0 : j0 + n], y[:])
            y_tiles[c] = y

        def y_quantize(c):
            j0, n = X_CHUNKS[c]
            woven = sb("y_woven%d" % c, [P, n, PACK], BF16)
            codes = sb("y_codes%d" % c, [P, n], U32)
            weave(woven[:], y_tiles[c][:])
            quantize(codes[:], y_scales[:, j0 : j0 + n], woven)
            nc.sync.dma_start(out_words[:, j0 : j0 + n], codes[:].bitcast(I32))

        chunks = len(X_CHUNKS)
        for step in range(chunks + 2):
            if step < chunks:
                x_quantize(step)
            if 0 <= step - 1 < chunks:
                combine(step - 1)
            if 0 <= step - 2 < chunks:
                y_quantize(step - 2)
        for q in range(4):
            engine = nc.sync if q % 2 else nc.scalar
            engine.dma_start(
                out_2[0, 4 * q : 4 * q + 4, :].bitcast(I32), y_scales[32 * q : 32 * q + 4, :].bitcast(I32)
            )
